import numpy as np
import ml_dtypes


def mxq(x, axis, fmt="e4m3"):
    dtype, down = {"e4m3": (ml_dtypes.float8_e4m3fn, 7), "e5m2": (ml_dtypes.float8_e5m2, 14)}[fmt]
    v = np.moveaxis(np.asarray(x, np.float32).astype(ml_dtypes.bfloat16).astype(np.float64), axis, -1)
    blocks = v.reshape(v.shape[:-1] + (-1, 32))
    amax = np.abs(blocks).max(-1, keepdims=True)
    byte = np.maximum(np.where(amax > 0, np.frexp(amax)[1] - 1 + 127, 0) - down, 1)
    scale = np.exp2(byte - 127.0)
    codes = (blocks / scale).astype(np.float32).astype(dtype).astype(np.float64)
    return np.moveaxis((codes * scale).reshape(v.shape), -1, axis)


WIDE = False


def mx_kscale(k):
    if not WIDE:
        return np.ones(k)
    levels = np.array([10, -10, 5, -5, 0])
    if k % 512:
        return np.exp2(np.random.permutation(np.resize(levels, k // 32))).repeat(32)
    a = np.empty((k // 512, 16))
    for p in range(k // 512):
        a[p, :8] = np.random.permutation(np.resize(levels, 8))
        for g in range(8):
            far = levels[np.abs(levels - a[p, g]) >= 10]
            a[p, g + 8] = far[np.random.randint(len(far))]
    return np.exp2(a.ravel()).repeat(32)


def f64(x):
    return np.asarray(x).astype(np.float64)


def striped(idx):
    return np.tile(idx.reshape(-1, 16).T, (8, 1)).astype(np.uint16)


def unstriped(offs):
    return offs[:16].T.reshape(-1).astype(np.int64)


E2M1 = np.array([0.0, 0.5, 1.0, 1.5, 2.0, 3.0, 4.0, 6.0, -0.0, -0.5, -1.0, -1.5, -2.0, -3.0, -4.0, -6.0])


def pack_weight(w, fmt):
    k, n = w.shape
    w = f64(np.asarray(w, np.float32).astype(ml_dtypes.bfloat16)).reshape(k // 32, 32, n)
    amax = np.abs(w).max(1)
    if fmt == "e4m3":
        byte = np.frexp(amax)[1] - 1 + 127 - 7
    else:
        mant, ex = np.frexp(amax / 6.0)
        byte = np.where(mant > 0.5, ex, ex - 1) + 127
    byte = np.clip(np.where(amax > 0, byte, 1), 1, 254)
    scaled = (w * np.exp2(127.0 - byte)[:, None, :]).reshape(k, n).astype(np.float32)
    by_word = np.ascontiguousarray(scaled.reshape(k // 512, 128, 4, n).transpose(0, 1, 3, 2))
    if fmt == "e4m3":
        words = by_word.astype(ml_dtypes.float8_e4m3fn).view(np.uint8)
    else:
        c = by_word.astype(ml_dtypes.float4_e2m1fn).view(np.uint8) & 0xF
        words = (c[..., 0::2] | (c[..., 1::2] << 4)).reshape(k // 512, 128, 2 * n)
    return np.ascontiguousarray(words), np.ascontiguousarray(byte.astype(np.uint8).reshape(k // 512, 16, n))


def unpack_weight(words, scales, fmt):
    g, _, n = scales.shape
    words = np.ascontiguousarray(words).reshape(g, 128, n, -1)
    if fmt == "e4m3":
        vals = words.view(ml_dtypes.float8_e4m3fn).astype(np.float64)
    else:
        nib = np.empty((g, 128, n, 4), np.uint8)
        nib[..., 0::2] = words & 0xF
        nib[..., 1::2] = words >> 4
        vals = E2M1[nib]
    vals = vals * np.repeat(np.exp2(scales.astype(np.float64) - 127.0), 8, axis=1)[..., None]
    return vals.transpose(0, 1, 3, 2).reshape(g * 512, n)


def gelu(v):
    return 0.5 * v * (1.0 + np.tanh(np.sqrt(2.0 / np.pi) * (v + 0.044715 * v**3)))


K, T, S, P, P2, H, N = 1024, 4096, 2048, 1024, 512, 512, 768

def setup_inputs():
    n = np.random.standard_normal
    s = mx_kscale(K)[:, None]
    u = mx_kscale(H)[:, None]
    tab_words, tab_scales = pack_weight(n((K, T)) * s, "e4m3")
    w1_words, w1_scales = pack_weight(1.5 * n((K, H)) / np.sqrt(K) / s, "e2m1")
    w4_words, w4_scales = pack_weight(n((H, N)) / np.sqrt(H) / u, "e4m3")
    return {
        "tab_words": tab_words, "tab_scales": tab_scales,
        "offs": striped(np.random.permutation(T)[:S]),
        "pos1": striped(np.random.permutation(S)[:P]),
        "pos2": striped(np.random.permutation(S)[:P]),
        "pos3": striped(np.random.permutation(P)[:P2]),
        "pos4": striped(np.random.permutation(S)[:P2]),
        "w1_words": w1_words, "w1_scales": w1_scales,
        "gain": (1.2 * np.exp(0.3 * n(H)) * u[:, 0]).astype(np.float32),
        "pgain": (1.2 * np.exp(0.3 * n(H)) / u[:, 0]).astype(np.float32),
        "w2": (n((H, N)) / np.sqrt(H) / u).astype(np.float32),
        "w3": (n((H, N)) / np.sqrt(H) / u).astype(np.float32),
        "w4_words": w4_words, "w4_scales": w4_scales,
    }

def reference(tab_words, tab_scales, offs, pos1, pos2, pos3, pos4, w1_words, w1_scales,
              gain, pgain, w2, w3, w4_words, w4_scales):
    v = unpack_weight(tab_words, tab_scales, "e4m3")[:, unstriped(offs)]
    w1 = unpack_weight(w1_words, w1_scales, "e2m1")
    w4 = unpack_weight(w4_words, w4_scales, "e4m3")
    h = f64(gain)[:, None] * np.tanh(w1.T @ v)
    a1 = f64(pgain)[:, None] * (h[:, unstriped(pos1)] * h[:, unstriped(pos2)])
    a2 = a1[:, unstriped(pos3)] - h[:, unstriped(pos4)]
    a2q = mxq(a2, 0, "e4m3")
    y2 = mxq(f64(w2), 0, "e4m3").T @ a2q
    y3 = mxq(f64(w3), 0, "e4m3").T @ a2q
    y4 = w4.T @ a2q
    return np.maximum(y2, y3) + y4

@@ -1,0 +1,286 @@
+from contextlib import ExitStack
+
+import concourse.mybir as mybir
+
+K, T, S, PAIRS, KEPT, H, N = 1024, 4096, 2048, 1024, 512, 512, 768
+FLOPS = 2 * K * H * S + 3 * 2 * H * N * KEPT
+
+F32 = mybir.dt.float32
+BF16 = mybir.dt.bfloat16
+I32 = mybir.dt.int32
+U32 = mybir.dt.uint32
+U16 = mybir.dt.uint16
+U8 = mybir.dt.uint8
+FP8X4 = mybir.dt.float8_e4m3fn_x4
+FP4X4 = mybir.dt.float4_e2m1fn_x4
+ALU = mybir.AluOpType
+ACT = mybir.ActivationFunctionType
+
+P = 128
+PACK = 4
+PASSES = K // (P * PACK)
+BANK = 512
+SLICES = S // BANK
+HALF_N = N // 2
+CHUNK = 128
+PER_COLUMN = 16
+
+
+def interleave_views(grouped, planes):
+    return (
+        grouped.rearrange("p (c i) t -> p c t i", i=4),
+        planes.rearrange("p t (c i) -> p c t i", i=4),
+    )
+
+
+def tile_list_tusk_pair_linking_kernel(
+    tc, tab_words, tab_scales, offs, pos1, pos2, pos3, pos4, w1_words, w1_scales,
+    gain, pgain, w2, w3, w4_words, w4_scales, out,
+):
+    nc = tc.nc
+    with ExitStack() as ctx:
+        lists = ctx.enter_context(tc.tile_pool(name="lists", bufs=1))
+        keep = ctx.enter_context(tc.tile_pool(name="keep", bufs=1))
+        ring = ctx.enter_context(tc.tile_pool(name="ring", bufs=2))
+        psum = ctx.enter_context(tc.psum_pool(name="psum", bufs=1))
+
+        def load_list(name, src):
+            tile = lists.tile(list(src.shape), U16, name=name)
+            nc.sync.dma_start(tile[:], src)
+            return tile
+
+        def zeroed_bytes(name, shape, tag=None):
+            tile = keep.tile(shape, U8, name=name, tag=tag or name, align_bytes=64)
+            flat = tile[:] if len(shape) == 2 else tile[:].rearrange("p a c -> p (a c)")
+            nc.vector.memset(flat.bitcast(I32), 0)
+            return tile
+
+        gain_t = keep.tile([P, PACK], F32, name="gain_t")
+        nc.gpsimd.dma_start(gain_t[:], gain.rearrange("(p t) -> p t", t=PACK))
+        pgain_t = keep.tile([P, PACK], F32, name="pgain_t")
+        nc.gpsimd.dma_start(pgain_t[:], pgain.rearrange("(p t) -> p t", t=PACK))
+        both_gains = keep.tile([P, PACK], F32, name="both_gains")
+        pair_gain = keep.tile([P, PACK], F32, name="pair_gain")
+        nc.gpsimd.tensor_tensor(both_gains[:], pgain_t[:], gain_t[:], ALU.mult)
+        nc.gpsimd.tensor_tensor(pair_gain[:], both_gains[:], gain_t[:], ALU.mult)
+        offs_t = load_list("offs_t", offs)
+        tab_sc = keep.tile([P, T], U8, name="tab_sc", tag="tab_sc")
+        nc.sync.dma_start(
+            tab_sc[:].bitcast(I32),
+            tab_scales.rearrange("a q t -> (a q) t").bitcast(I32).unsqueeze(1).broadcast_to([32, 4, T // 4]),
+        )
+        w1_raw = keep.tile([P, PASSES, 2 * H], U8, name="w1_raw", tag="stage")
+        nc.sync.dma_start(w1_raw[:].bitcast(I32), w1_words.rearrange("a p c -> p a c").bitcast(I32))
+        tab = [keep.tile([P, T], I32, name=f"tab{a}", tag=f"tab{a}", align_bytes=64) for a in range(PASSES)]
+        nc.sync.dma_start(tab[0][:], tab_words[0].rearrange("p t i -> p (t i)").bitcast(I32))
+        w1_sc_raw = zeroed_bytes("w1_sc_raw", [P, PASSES, H])
+        for quad in range(4):
+            nc.sync.dma_start(
+                w1_sc_raw[32 * quad : 32 * quad + 4, :, :].bitcast(I32),
+                w1_scales[:, 4 * quad : 4 * quad + 4, :].rearrange("a r c -> r a c").bitcast(I32),
+            )
+        nc.sync.dma_start(tab[1][:], tab_words[1].rearrange("p t i -> p (t i)").bitcast(I32))
+        v_sc = [zeroed_bytes(f"v_sc{a}", [P, S]) for a in range(PASSES)]
+
+        w1_words_by_t = w1_raw[:].bitcast(U16).rearrange("p a (q t) -> p a t q", t=PACK)
+        w1_sc_by_t = w1_sc_raw[:].rearrange("p a (q t) -> p a t q", t=PACK)
+        first_codes = keep.tile([P, PASSES, 1, 2 * P], U8, name="first_codes", align_bytes=64)
+        nc.vector.tensor_copy(first_codes[:].bitcast(U16), w1_words_by_t[:, :, 0:1, :])
+
+        picked_sc = keep.tile([P, S], U8, name="picked_sc", tag="picked_sc")
+        nc.vector.tensor_copy(picked_sc[:], tab_sc[:].indirect(offs_t[:]))
+        for a in range(PASSES):
+            for quad in range(4):
+                first = 4 * (16 * a + 4 * quad)
+                nc.sync.dma_start(
+                    v_sc[a][32 * quad : 32 * quad + 4, :].bitcast(I32),
+                    picked_sc[first : first + 13 : 4, :].bitcast(I32),
+                )
+        first_sc = keep.tile([P, PASSES, 1, P], U8, name="first_sc", align_bytes=64)
+        nc.vector.tensor_copy(first_sc[:], w1_sc_by_t[:, :, 0:1, :])
+        w1_codes = {0: first_codes[:, :, 0, :]}
+        w1_sc = {0: first_sc[:, :, 0, :]}
+
+        v0 = keep.tile([P, S], U32, name="v0", tag="v0", align_bytes=64)
+        nc.vector.tensor_copy(v0[:], tab[0][:].bitcast(U32).indirect(offs_t[:]))
+
+        step = BANK // PER_COLUMN
+        v1 = [keep.tile([P, BANK], U32, name=f"v1_{s}", align_bytes=64) for s in range(SLICES)]
+        for s in range(SLICES):
+            nc.vector.tensor_copy(v1[s][:], tab[1][:].bitcast(U32).indirect(offs_t[:, s * step : (s + 1) * step]))
+
+        pos1_t = load_list("pos1_t", pos1)
+        pos4_t = load_list("pos4_t", pos4)
+        pos2_t = load_list("pos2_t", pos2)
+        pos3_t = load_list("pos3_t", pos3)
+        w_raw = {}
+
+        def load_weights(piece, tag, align):
+            src = (w2, w3)[piece % 2][:, (piece // 2) * HALF_N : (piece // 2 + 1) * HALF_N]
+            raw = keep.tile([P, PACK, HALF_N], F32, name=f"w_raw{piece}", tag=tag, align_bytes=align)
+            nc.sync.dma_start(raw[:], src.rearrange("(p t) n -> p t n", t=PACK))
+            w_raw[piece] = raw
+
+
+        traits = [keep.tile([P, S], F32, name=f"traits{t}") for t in range(PACK)]
+
+        def first_pass(bank, t, s, a):
+            cols = slice(s * BANK, (s + 1) * BANK)
+            words = v0[:, cols] if a == 0 else v1[s][:]
+            nc.tensor.matmul_mx(
+                bank[:],
+                lhsT=w1_codes[t][:, a, :].bitcast(FP4X4),
+                lhsT_scale=w1_sc[t][:, a, :],
+                rhs=words.bitcast(FP8X4),
+                rhs_scale=v_sc[a][:, cols],
+                start=(a == 0),
+                stop=(a == PASSES - 1),
+            )
+
+        def tanh_out(bank, t, s):
+            nc.scalar.activation(traits[t][:, s * BANK : (s + 1) * BANK], bank[:], ACT.Tanh)
+
+        for s in range(SLICES):
+            bank = psum.tile([P, BANK], F32, name=f"bank{s}")
+            for a in range(PASSES):
+                first_pass(bank, 0, s, a)
+            tanh_out(bank, 0, s)
+
+        w_codes = [keep.tile([P, HALF_N], U32, name=f"w_codes{i}", align_bytes=64) for i in range(4)]
+        w_sc = [keep.tile([P, HALF_N], U8, name=f"w_sc{i}", align_bytes=64) for i in range(4)]
+
+        def round_weights(piece, copy):
+            grouped = ring.tile([P, HALF_N, PACK], BF16, name="w_grouped", align_bytes=64)
+            dst, src = interleave_views(grouped[:], w_raw[piece][:])
+            copy(dst, src)
+            return grouped
+
+        def quantize_weights(piece, grouped):
+            nc.vector.quantize_mx(
+                w_codes[piece][:].bitcast(FP8X4), w_sc[piece][:], grouped[:].rearrange("p c t -> p (c t)")
+            )
+
+        rest = PACK - 1
+        later = keep.tile([P, PASSES * rest * 3 * P], U8, name="later", tag="tab1", align_bytes=64)
+        split = PASSES * rest * 2 * P
+        later_codes = later[:, 0:split].rearrange("p (a t c) -> p a t c", a=PASSES, t=rest)
+        later_sc = later[:, split:].rearrange("p (a t c) -> p a t c", a=PASSES, t=rest)
+        nc.vector.tensor_copy(later_codes.bitcast(U16), w1_words_by_t[:, :, 1:PACK, :])
+        nc.vector.tensor_copy(later_sc, w1_sc_by_t[:, :, 1:PACK, :])
+        for t in range(1, PACK):
+            w1_codes[t] = later_codes[:, :, t - 1, :]
+            w1_sc[t] = later_sc[:, :, t - 1, :]
+        w4_sc = zeroed_bytes("w4_sc", [P, N], tag="w1_sc_raw")
+        for quad in range(4):
+            nc.sync.dma_start(
+                w4_sc[32 * quad : 32 * quad + 4, :].bitcast(I32),
+                w4_scales[0, 4 * quad : 4 * quad + 4, :].bitcast(I32),
+            )
+        w4_codes = keep.tile([P, N], I32, name="w4_codes", tag="tab0", align_bytes=64)
+        nc.sync.dma_start(w4_codes[:], w4_words[0].rearrange("p c i -> p (c i)").bitcast(I32))
+
+        pairs = [keep.tile([P, PAIRS], F32, name=f"pairs{t}") for t in range(PACK)]
+        site = [keep.tile([P, KEPT], F32, name=f"site{t}") for t in range(PACK)]
+        for t in range(PACK):
+            nxt = t + 1
+            load_weights(t, "stage", None)
+            if nxt < PACK:
+                for s in range(SLICES):
+                    bank = psum.tile([P, BANK], F32, name=f"bank{s}")
+                    for a in range(PASSES):
+                        first_pass(bank, nxt, s, a)
+                    tanh_out(bank, nxt, s)
+            left = []
+            for u in range(2):
+                g = ring.tile([P, BANK], F32, name="left", bufs=4)
+                nc.vector.tensor_copy(g[:], traits[t][:].indirect(pos1_t[:, u * step : (u + 1) * step]))
+                nc.scalar.activation(g[:], g[:], ACT.Copy, scale=pair_gain[:, t : t + 1])
+                left.append(g)
+            nc.vector.tensor_copy(site[t][:], traits[t][:].indirect(pos4_t[:]))
+            nc.scalar.activation(site[t][:], site[t][:], ACT.Copy, scale=gain_t[:, t : t + 1])
+            grouped = round_weights(t, nc.scalar.copy)
+            for u in range(2):
+                nc.vector.tensor_tensor(
+                    pairs[t][:, u * BANK : (u + 1) * BANK],
+                    traits[t][:].indirect(pos2_t[:, u * step : (u + 1) * step]),
+                    left[u][:],
+                    ALU.mult,
+                )
+            quantize_weights(t, grouped)
+
+        out_v = out.rearrange("(m p) j -> p m j", p=P)
+        chunks = KEPT // CHUNK
+        cstep = CHUNK // PER_COLUMN
+
+        def kept(c):
+            planes = ring.tile([P, PACK, CHUNK], F32, name="kept_planes")
+            for t in range(PACK):
+                nc.vector.tensor_tensor(
+                    planes[:, t, :],
+                    pairs[t][:].indirect(pos3_t[:, c * cstep : (c + 1) * cstep]),
+                    site[t][:, c * CHUNK : (c + 1) * CHUNK],
+                    ALU.subtract,
+                )
+            grouped = ring.tile([P, CHUNK, PACK], BF16, name="kept_grouped", align_bytes=64)
+            dst, src = interleave_views(grouped[:], planes[:])
+            if c < chunks - 1:
+                nc.scalar.copy(dst, src)
+            else:
+                nc.vector.tensor_copy(dst, src)
+            return grouped
+
+        def scores(c, grouped):
+            codes = ring.tile([P, CHUNK], U32, name="kept_codes", align_bytes=64)
+            scales = ring.tile([P, CHUNK], U8, name="kept_sc", align_bytes=64)
+            nc.vector.quantize_mx(codes[:].bitcast(FP8X4), scales[:], grouped[:].rearrange("p c t -> p (c t)"))
+            banks = []
+            for half in range(2):
+                trio = []
+                for which in range(3):
+                    bank = psum.tile([P, BANK], F32, name=f"bank{(6 * c + 3 * half + which) % 8}")
+                    for m in range(3):
+                        if which < 2:
+                            piece = 2 * half + which
+                            cols = slice(m * P, (m + 1) * P)
+                            lhs, lhs_sc = w_codes[piece][:, cols], w_sc[piece][:, cols]
+                        else:
+                            cols = slice(half * HALF_N + m * P, half * HALF_N + (m + 1) * P)
+                            lhs, lhs_sc = w4_codes[:, cols], w4_sc[:, cols]
+                        nc.tensor.matmul_mx(
+                            bank[:, m * CHUNK : (m + 1) * CHUNK],
+                            lhsT=lhs.bitcast(FP8X4),
+                            lhsT_scale=lhs_sc,
+                            rhs=codes[:].bitcast(FP8X4),
+                            rhs_scale=scales[:],
+                            start=True,
+                            stop=True,
+                        )
+                    trio.append(bank)
+                banks.append(trio)
+            return banks
+
+        def finish(c, banks):
+            width = 3 * CHUNK
+            larger = []
+            for half in range(2):
+                y2 = ring.tile([P, width], F32, name="y2")
+                nc.scalar.copy(y2[:], banks[half][0][:, 0:width])
+                best = ring.tile([P, width], F32, name="best")
+                nc.vector.tensor_tensor(best[:], banks[half][1][:, 0:width], y2[:], ALU.max)
+                larger.append(best)
+            for half in range(2):
+                result = ring.tile([P, 3, CHUNK], F32, name="result", bufs=4)
+                nc.vector.tensor_tensor(
+                    result[:].rearrange("p m j -> p (m j)"), banks[half][2][:, 0:width], larger[half][:], ALU.add
+                )
+                nc.sync.dma_start(out_v[:, 3 * half : 3 * half + 3, c * CHUNK : (c + 1) * CHUNK], result[:])
+
+        grouped = {0: kept(0)}
+        banks = {}
+        for c in range(chunks):
+            if c + 1 < chunks:
+                grouped[c + 1] = kept(c + 1)
+            if c > 0:
+                finish(c - 1, banks[c - 1])
+            banks[c] = scores(c, grouped[c])
+        finish(chunks - 1, banks[chunks - 1])

@@ -27,10 +27,7 @@ PER_COLUMN = 16
 
 
 def interleave_views(grouped, planes):
-    return (
-        grouped.rearrange("p (c i) t -> p c t i", i=4),
-        planes.rearrange("p t (c i) -> p c t i", i=4),
-    )
+    return grouped, planes.rearrange("p t c -> p c t")
 
 
 def tile_list_tusk_pair_linking_kernel(
@@ -55,21 +52,23 @@ def tile_list_tusk_pair_linking_kernel(
             nc.vector.memset(flat.bitcast(I32), 0)
             return tile
 
+        tab_sc = keep.tile([P, T], U8, name="tab_sc", tag="tab_sc")
+        nc.sync.dma_start(
+            tab_sc[:].bitcast(I32),
+            tab_scales.rearrange("a q t -> (a q) t").bitcast(I32).unsqueeze(1).broadcast_to([32, 4, T // 4]),
+        )
         gain_t = keep.tile([P, PACK], F32, name="gain_t")
         nc.gpsimd.dma_start(gain_t[:], gain.rearrange("(p t) -> p t", t=PACK))
         pgain_t = keep.tile([P, PACK], F32, name="pgain_t")
         nc.gpsimd.dma_start(pgain_t[:], pgain.rearrange("(p t) -> p t", t=PACK))
         both_gains = keep.tile([P, PACK], F32, name="both_gains")
         pair_gain = keep.tile([P, PACK], F32, name="pair_gain")
-        nc.gpsimd.tensor_tensor(both_gains[:], pgain_t[:], gain_t[:], ALU.mult)
-        nc.gpsimd.tensor_tensor(pair_gain[:], both_gains[:], gain_t[:], ALU.mult)
+        for t in range(PACK):
+            nc.scalar.activation(both_gains[:, t : t + 1], pgain_t[:, t : t + 1], ACT.Copy, scale=gain_t[:, t : t + 1])
+        for t in range(PACK):
+            nc.scalar.activation(pair_gain[:, t : t + 1], both_gains[:, t : t + 1], ACT.Copy, scale=gain_t[:, t : t + 1])
         offs_t = load_list("offs_t", offs)
-        tab_sc = keep.tile([P, T], U8, name="tab_sc", tag="tab_sc")
-        nc.sync.dma_start(
-            tab_sc[:].bitcast(I32),
-            tab_scales.rearrange("a q t -> (a q) t").bitcast(I32).unsqueeze(1).broadcast_to([32, 4, T // 4]),
-        )
-        w1_raw = keep.tile([P, PASSES, 2 * H], U8, name="w1_raw", tag="stage")
+        w1_raw = keep.tile([P, PASSES, 2 * H], U8, name="w1_raw")
         nc.sync.dma_start(w1_raw[:].bitcast(I32), w1_words.rearrange("a p c -> p a c").bitcast(I32))
         tab = [keep.tile([P, T], I32, name=f"tab{a}", tag=f"tab{a}", align_bytes=64) for a in range(PASSES)]
         nc.sync.dma_start(tab[0][:], tab_words[0].rearrange("p t i -> p (t i)").bitcast(I32))
@@ -113,13 +112,14 @@ def tile_list_tusk_pair_linking_kernel(
         pos4_t = load_list("pos4_t", pos4)
         pos2_t = load_list("pos2_t", pos2)
         pos3_t = load_list("pos3_t", pos3)
-        w_raw = {}
-
-        def load_weights(piece, tag, align):
+        w4_codes = keep.tile([P, N], I32, name="w4_codes", align_bytes=64)
+        nc.sync.dma_start(w4_codes[:], w4_words[0].rearrange("p c i -> p (c i)").bitcast(I32))
+        w_raw = []
+        for piece in range(4):
             src = (w2, w3)[piece % 2][:, (piece // 2) * HALF_N : (piece // 2 + 1) * HALF_N]
-            raw = keep.tile([P, PACK, HALF_N], F32, name=f"w_raw{piece}", tag=tag, align_bytes=align)
+            raw = keep.tile([P, PACK, HALF_N], F32, name=f"w_raw{piece}")
             nc.sync.dma_start(raw[:], src.rearrange("(p t) n -> p t n", t=PACK))
-            w_raw[piece] = raw
+            w_raw.append(raw)
 
 
         traits = [keep.tile([P, S], F32, name=f"traits{t}") for t in range(PACK)]
@@ -176,14 +176,11 @@ def tile_list_tusk_pair_linking_kernel(
                 w4_sc[32 * quad : 32 * quad + 4, :].bitcast(I32),
                 w4_scales[0, 4 * quad : 4 * quad + 4, :].bitcast(I32),
             )
-        w4_codes = keep.tile([P, N], I32, name="w4_codes", tag="tab0", align_bytes=64)
-        nc.sync.dma_start(w4_codes[:], w4_words[0].rearrange("p c i -> p (c i)").bitcast(I32))
 
         pairs = [keep.tile([P, PAIRS], F32, name=f"pairs{t}") for t in range(PACK)]
         site = [keep.tile([P, KEPT], F32, name=f"site{t}") for t in range(PACK)]
         for t in range(PACK):
             nxt = t + 1
-            load_weights(t, "stage", None)
             if nxt < PACK:
                 for s in range(SLICES):
                     bank = psum.tile([P, BANK], F32, name=f"bank{s}")

@@ -62,11 +62,15 @@ def tile_list_tusk_pair_linking_kernel(
         pgain_t = keep.tile([P, PACK], F32, name="pgain_t")
         nc.gpsimd.dma_start(pgain_t[:], pgain.rearrange("(p t) -> p t", t=PACK))
         both_gains = keep.tile([P, PACK], F32, name="both_gains")
-        pair_gain = keep.tile([P, PACK], F32, name="pair_gain")
+        pair_gain = [keep.tile([P, BANK], F32, name=f"pair_gain{t}") for t in range(PACK)]
+        site_gain = [keep.tile([P, KEPT], F32, name=f"site_gain{t}") for t in range(PACK)]
         for t in range(PACK):
             nc.scalar.activation(both_gains[:, t : t + 1], pgain_t[:, t : t + 1], ACT.Copy, scale=gain_t[:, t : t + 1])
         for t in range(PACK):
-            nc.scalar.activation(pair_gain[:, t : t + 1], both_gains[:, t : t + 1], ACT.Copy, scale=gain_t[:, t : t + 1])
+            nc.scalar.activation(
+                pair_gain[t][:], both_gains[:, t : t + 1].to_broadcast([P, BANK]), ACT.Copy, scale=gain_t[:, t : t + 1]
+            )
+            nc.scalar.copy(site_gain[t][:], gain_t[:, t : t + 1].to_broadcast([P, KEPT]))
         offs_t = load_list("offs_t", offs)
         w1_raw = keep.tile([P, PASSES, 2 * H], U8, name="w1_raw")
         nc.sync.dma_start(w1_raw[:].bitcast(I32), w1_words.rearrange("a p c -> p a c").bitcast(I32))
@@ -187,22 +191,17 @@ def tile_list_tusk_pair_linking_kernel(
                     for a in range(PASSES):
                         first_pass(bank, nxt, s, a)
                     tanh_out(bank, nxt, s)
-            left = []
-            for u in range(2):
-                g = ring.tile([P, BANK], F32, name="left", bufs=4)
-                nc.vector.tensor_copy(g[:], traits[t][:].indirect(pos1_t[:, u * step : (u + 1) * step]))
-                nc.scalar.activation(g[:], g[:], ACT.Copy, scale=pair_gain[:, t : t + 1])
-                left.append(g)
-            nc.vector.tensor_copy(site[t][:], traits[t][:].indirect(pos4_t[:]))
-            nc.scalar.activation(site[t][:], site[t][:], ACT.Copy, scale=gain_t[:, t : t + 1])
-            grouped = round_weights(t, nc.scalar.copy)
+            left = ring.tile([P, PAIRS], F32, name="left")
             for u in range(2):
                 nc.vector.tensor_tensor(
-                    pairs[t][:, u * BANK : (u + 1) * BANK],
-                    traits[t][:].indirect(pos2_t[:, u * step : (u + 1) * step]),
-                    left[u][:],
+                    left[:, u * BANK : (u + 1) * BANK],
+                    traits[t][:].indirect(pos1_t[:, u * step : (u + 1) * step]),
+                    pair_gain[t][:],
                     ALU.mult,
                 )
+            nc.vector.tensor_tensor(site[t][:], traits[t][:].indirect(pos4_t[:]), site_gain[t][:], ALU.mult)
+            grouped = round_weights(t, nc.scalar.copy)
+            nc.vector.tensor_tensor(pairs[t][:], traits[t][:].indirect(pos2_t[:]), left[:], ALU.mult)
             quantize_weights(t, grouped)
 
         out_v = out.rearrange("(m p) j -> p m j", p=P)

@@ -53,29 +53,28 @@ def tile_list_tusk_pair_linking_kernel(
             return tile
 
         tab_sc = keep.tile([P, T], U8, name="tab_sc", tag="tab_sc")
-        nc.sync.dma_start(
-            tab_sc[:].bitcast(I32),
-            tab_scales.rearrange("a q t -> (a q) t").bitcast(I32).unsqueeze(1).broadcast_to([32, 4, T // 4]),
-        )
+        nc.sync.dma_start(tab_sc[0:32, :].bitcast(I32), tab_scales.rearrange("a q t -> (a q) t").bitcast(I32))
+        nc.vector.memset(tab_sc[32:64, :].bitcast(I32), 0)
+        nc.gpsimd.memset(tab_sc[64:P, :].bitcast(I32), 0)
+        offs_t = load_list("offs_t", offs)
         gain_t = keep.tile([P, PACK], F32, name="gain_t")
-        nc.gpsimd.dma_start(gain_t[:], gain.rearrange("(p t) -> p t", t=PACK))
+        nc.sync.dma_start(gain_t[:], gain.rearrange("(p t) -> p t", t=PACK))
         pgain_t = keep.tile([P, PACK], F32, name="pgain_t")
-        nc.gpsimd.dma_start(pgain_t[:], pgain.rearrange("(p t) -> p t", t=PACK))
+        nc.sync.dma_start(pgain_t[:], pgain.rearrange("(p t) -> p t", t=PACK))
         both_gains = keep.tile([P, PACK], F32, name="both_gains")
-        pair_gain = [keep.tile([P, BANK], F32, name=f"pair_gain{t}") for t in range(PACK)]
+        pair_gain = [keep.tile([P, PAIRS], F32, name=f"pair_gain{t}") for t in range(PACK)]
         site_gain = [keep.tile([P, KEPT], F32, name=f"site_gain{t}") for t in range(PACK)]
         for t in range(PACK):
             nc.scalar.activation(both_gains[:, t : t + 1], pgain_t[:, t : t + 1], ACT.Copy, scale=gain_t[:, t : t + 1])
         for t in range(PACK):
             nc.scalar.activation(
-                pair_gain[t][:], both_gains[:, t : t + 1].to_broadcast([P, BANK]), ACT.Copy, scale=gain_t[:, t : t + 1]
+                pair_gain[t][:], both_gains[:, t : t + 1].to_broadcast([P, PAIRS]), ACT.Copy, scale=gain_t[:, t : t + 1]
             )
             nc.scalar.copy(site_gain[t][:], gain_t[:, t : t + 1].to_broadcast([P, KEPT]))
-        offs_t = load_list("offs_t", offs)
         w1_raw = keep.tile([P, PASSES, 2 * H], U8, name="w1_raw")
-        nc.sync.dma_start(w1_raw[:].bitcast(I32), w1_words.rearrange("a p c -> p a c").bitcast(I32))
         tab = [keep.tile([P, T], I32, name=f"tab{a}", tag=f"tab{a}", align_bytes=64) for a in range(PASSES)]
         nc.sync.dma_start(tab[0][:], tab_words[0].rearrange("p t i -> p (t i)").bitcast(I32))
+        nc.sync.dma_start(w1_raw[:].bitcast(I32), w1_words.rearrange("a p c -> p a c").bitcast(I32))
         w1_sc_raw = zeroed_bytes("w1_sc_raw", [P, PASSES, H])
         for quad in range(4):
             nc.sync.dma_start(
@@ -87,18 +86,18 @@ def tile_list_tusk_pair_linking_kernel(
 
         w1_words_by_t = w1_raw[:].bitcast(U16).rearrange("p a (q t) -> p a t q", t=PACK)
         w1_sc_by_t = w1_sc_raw[:].rearrange("p a (q t) -> p a t q", t=PACK)
-        first_codes = keep.tile([P, PASSES, 1, 2 * P], U8, name="first_codes", align_bytes=64)
-        nc.vector.tensor_copy(first_codes[:].bitcast(U16), w1_words_by_t[:, :, 0:1, :])
 
         picked_sc = keep.tile([P, S], U8, name="picked_sc", tag="picked_sc")
         nc.vector.tensor_copy(picked_sc[:], tab_sc[:].indirect(offs_t[:]))
         for a in range(PASSES):
             for quad in range(4):
-                first = 4 * (16 * a + 4 * quad)
+                first = 16 * a + 4 * quad
                 nc.sync.dma_start(
                     v_sc[a][32 * quad : 32 * quad + 4, :].bitcast(I32),
-                    picked_sc[first : first + 13 : 4, :].bitcast(I32),
+                    picked_sc[first : first + 4, :].bitcast(I32),
                 )
+        first_codes = keep.tile([P, PASSES, 1, 2 * P], U8, name="first_codes", align_bytes=64)
+        nc.vector.tensor_copy(first_codes[:].bitcast(U16), w1_words_by_t[:, :, 0:1, :])
         first_sc = keep.tile([P, PASSES, 1, P], U8, name="first_sc", align_bytes=64)
         nc.vector.tensor_copy(first_sc[:], w1_sc_by_t[:, :, 0:1, :])
         w1_codes = {0: first_codes[:, :, 0, :]}
@@ -192,13 +191,7 @@ def tile_list_tusk_pair_linking_kernel(
                         first_pass(bank, nxt, s, a)
                     tanh_out(bank, nxt, s)
             left = ring.tile([P, PAIRS], F32, name="left")
-            for u in range(2):
-                nc.vector.tensor_tensor(
-                    left[:, u * BANK : (u + 1) * BANK],
-                    traits[t][:].indirect(pos1_t[:, u * step : (u + 1) * step]),
-                    pair_gain[t][:],
-                    ALU.mult,
-                )
+            nc.vector.tensor_tensor(left[:], traits[t][:].indirect(pos1_t[:]), pair_gain[t][:], ALU.mult)
             nc.vector.tensor_tensor(site[t][:], traits[t][:].indirect(pos4_t[:]), site_gain[t][:], ALU.mult)
             grouped = round_weights(t, nc.scalar.copy)
             nc.vector.tensor_tensor(pairs[t][:], traits[t][:].indirect(pos2_t[:]), left[:], ALU.mult)

@@ -17,17 +17,21 @@ ALU = mybir.AluOpType
 ACT = mybir.ActivationFunctionType
 
 P = 128
+QUAD = 32
+QUADS = P // QUAD
+SCALE_ROWS = 4
 PACK = 4
 PASSES = K // (P * PACK)
 BANK = 512
+BANKS = 8
 SLICES = S // BANK
-HALF_N = N // 2
-CHUNK = 128
 PER_COLUMN = 16
-
-
-def interleave_views(grouped, planes):
-    return grouped, planes.rearrange("p t c -> p c t")
+HALF_N = N // 2
+HALF_TILES = HALF_N // P
+PIECES = 4
+CHUNK = 128
+CHUNKS = KEPT // CHUNK
+SCORE_ORDER = [(half, w) for half in range(2) for w in range(2)] + [(half, 2) for half in range(2)]
 
 
 def tile_list_tusk_pair_linking_kernel(
@@ -46,17 +50,21 @@ def tile_list_tusk_pair_linking_kernel(
             nc.sync.dma_start(tile[:], src)
             return tile
 
-        def zeroed_bytes(name, shape, tag=None):
-            tile = keep.tile(shape, U8, name=name, tag=tag or name, align_bytes=64)
+        def zeroed_scales(name, shape, tag):
+            tile = keep.tile(shape, U8, name=name, tag=tag, align_bytes=64)
             flat = tile[:] if len(shape) == 2 else tile[:].rearrange("p a c -> p (a c)")
             nc.vector.memset(flat.bitcast(I32), 0)
             return tile
 
-        tab_sc = keep.tile([P, T], U8, name="tab_sc", tag="tab_sc")
-        nc.sync.dma_start(tab_sc[0:32, :].bitcast(I32), tab_scales.rearrange("a q t -> (a q) t").bitcast(I32))
-        nc.vector.memset(tab_sc[32:64, :].bitcast(I32), 0)
-        nc.gpsimd.memset(tab_sc[64:P, :].bitcast(I32), 0)
+        def scale_rows(quad):
+            return slice(QUAD * quad, QUAD * quad + SCALE_ROWS)
+
+        tab_sc = keep.tile([P, T], U8, name="tab_sc")
+        nc.sync.dma_start(tab_sc[0:QUAD, :].bitcast(I32), tab_scales.rearrange("a q t -> (a q) t").bitcast(I32))
+        nc.vector.memset(tab_sc[QUAD : 2 * QUAD, :].bitcast(I32), 0)
+        nc.gpsimd.memset(tab_sc[2 * QUAD : P, :].bitcast(I32), 0)
         offs_t = load_list("offs_t", offs)
+
         gain_t = keep.tile([P, PACK], F32, name="gain_t")
         nc.sync.dma_start(gain_t[:], gain.rearrange("(p t) -> p t", t=PACK))
         pgain_t = keep.tile([P, PACK], F32, name="pgain_t")
@@ -71,45 +79,45 @@ def tile_list_tusk_pair_linking_kernel(
                 pair_gain[t][:], both_gains[:, t : t + 1].to_broadcast([P, PAIRS]), ACT.Copy, scale=gain_t[:, t : t + 1]
             )
             nc.scalar.copy(site_gain[t][:], gain_t[:, t : t + 1].to_broadcast([P, KEPT]))
+
         w1_raw = keep.tile([P, PASSES, 2 * H], U8, name="w1_raw")
         tab = [keep.tile([P, T], I32, name=f"tab{a}", tag=f"tab{a}", align_bytes=64) for a in range(PASSES)]
         nc.sync.dma_start(tab[0][:], tab_words[0].rearrange("p t i -> p (t i)").bitcast(I32))
         nc.sync.dma_start(w1_raw[:].bitcast(I32), w1_words.rearrange("a p c -> p a c").bitcast(I32))
-        w1_sc_raw = zeroed_bytes("w1_sc_raw", [P, PASSES, H])
-        for quad in range(4):
+        w1_sc_raw = zeroed_scales("w1_sc_raw", [P, PASSES, H], "w1_sc_raw")
+        for quad in range(QUADS):
+            rows = w1_scales[:, SCALE_ROWS * quad : SCALE_ROWS * (quad + 1), :]
             nc.sync.dma_start(
-                w1_sc_raw[32 * quad : 32 * quad + 4, :, :].bitcast(I32),
-                w1_scales[:, 4 * quad : 4 * quad + 4, :].rearrange("a r c -> r a c").bitcast(I32),
+                w1_sc_raw[scale_rows(quad), :, :].bitcast(I32), rows.rearrange("a i c -> i a c").bitcast(I32)
             )
         nc.sync.dma_start(tab[1][:], tab_words[1].rearrange("p t i -> p (t i)").bitcast(I32))
-        v_sc = [zeroed_bytes(f"v_sc{a}", [P, S]) for a in range(PASSES)]
+        v_sc = [zeroed_scales(f"v_sc{a}", [P, S], f"v_sc{a}") for a in range(PASSES)]
 
-        w1_words_by_t = w1_raw[:].bitcast(U16).rearrange("p a (q t) -> p a t q", t=PACK)
-        w1_sc_by_t = w1_sc_raw[:].rearrange("p a (q t) -> p a t q", t=PACK)
-
-        picked_sc = keep.tile([P, S], U8, name="picked_sc", tag="picked_sc")
+        picked_sc = keep.tile([P, S], U8, name="picked_sc")
         nc.vector.tensor_copy(picked_sc[:], tab_sc[:].indirect(offs_t[:]))
         for a in range(PASSES):
-            for quad in range(4):
-                first = 16 * a + 4 * quad
+            for quad in range(QUADS):
+                row = SCALE_ROWS * (QUADS * a + quad)
                 nc.sync.dma_start(
-                    v_sc[a][32 * quad : 32 * quad + 4, :].bitcast(I32),
-                    picked_sc[first : first + 4, :].bitcast(I32),
+                    v_sc[a][scale_rows(quad), :].bitcast(I32), picked_sc[row : row + SCALE_ROWS, :].bitcast(I32)
                 )
+
+        w1_words_by_slot = w1_raw[:].bitcast(U16).rearrange("p a (q t) -> p a t q", t=PACK)
+        w1_sc_by_slot = w1_sc_raw[:].rearrange("p a (q t) -> p a t q", t=PACK)
         first_codes = keep.tile([P, PASSES, 1, 2 * P], U8, name="first_codes", align_bytes=64)
-        nc.vector.tensor_copy(first_codes[:].bitcast(U16), w1_words_by_t[:, :, 0:1, :])
+        nc.vector.tensor_copy(first_codes[:].bitcast(U16), w1_words_by_slot[:, :, 0:1, :])
         first_sc = keep.tile([P, PASSES, 1, P], U8, name="first_sc", align_bytes=64)
-        nc.vector.tensor_copy(first_sc[:], w1_sc_by_t[:, :, 0:1, :])
+        nc.vector.tensor_copy(first_sc[:], w1_sc_by_slot[:, :, 0:1, :])
         w1_codes = {0: first_codes[:, :, 0, :]}
         w1_sc = {0: first_sc[:, :, 0, :]}
 
-        v0 = keep.tile([P, S], U32, name="v0", tag="v0", align_bytes=64)
+        v0 = keep.tile([P, S], U32, name="v0", align_bytes=64)
         nc.vector.tensor_copy(v0[:], tab[0][:].bitcast(U32).indirect(offs_t[:]))
-
-        step = BANK // PER_COLUMN
+        slice_columns = BANK // PER_COLUMN
         v1 = [keep.tile([P, BANK], U32, name=f"v1_{s}", align_bytes=64) for s in range(SLICES)]
         for s in range(SLICES):
-            nc.vector.tensor_copy(v1[s][:], tab[1][:].bitcast(U32).indirect(offs_t[:, s * step : (s + 1) * step]))
+            slice_offs = offs_t[:, s * slice_columns : (s + 1) * slice_columns]
+            nc.vector.tensor_copy(v1[s][:], tab[1][:].bitcast(U32).indirect(slice_offs))
 
         pos1_t = load_list("pos1_t", pos1)
         pos4_t = load_list("pos4_t", pos4)
@@ -118,158 +126,131 @@ def tile_list_tusk_pair_linking_kernel(
         w4_codes = keep.tile([P, N], I32, name="w4_codes", align_bytes=64)
         nc.sync.dma_start(w4_codes[:], w4_words[0].rearrange("p c i -> p (c i)").bitcast(I32))
         w_raw = []
-        for piece in range(4):
-            src = (w2, w3)[piece % 2][:, (piece // 2) * HALF_N : (piece // 2 + 1) * HALF_N]
+        for piece in range(PIECES):
+            half, w = divmod(piece, 2)
+            src = (w2, w3)[w][:, half * HALF_N : (half + 1) * HALF_N]
             raw = keep.tile([P, PACK, HALF_N], F32, name=f"w_raw{piece}")
             nc.sync.dma_start(raw[:], src.rearrange("(p t) n -> p t n", t=PACK))
             w_raw.append(raw)
 
-
         traits = [keep.tile([P, S], F32, name=f"traits{t}") for t in range(PACK)]
 
-        def first_pass(bank, t, s, a):
-            cols = slice(s * BANK, (s + 1) * BANK)
-            words = v0[:, cols] if a == 0 else v1[s][:]
-            nc.tensor.matmul_mx(
-                bank[:],
-                lhsT=w1_codes[t][:, a, :].bitcast(FP4X4),
-                lhsT_scale=w1_sc[t][:, a, :],
-                rhs=words.bitcast(FP8X4),
-                rhs_scale=v_sc[a][:, cols],
-                start=(a == 0),
-                stop=(a == PASSES - 1),
-            )
+        def first_product(t):
+            for s in range(SLICES):
+                cols = slice(s * BANK, (s + 1) * BANK)
+                bank = psum.tile([P, BANK], F32, name=f"bank{s}")
+                for a, words in enumerate((v0[:, cols], v1[s][:])):
+                    nc.tensor.matmul_mx(
+                        bank[:],
+                        lhsT=w1_codes[t][:, a, :].bitcast(FP4X4),
+                        lhsT_scale=w1_sc[t][:, a, :],
+                        rhs=words.bitcast(FP8X4),
+                        rhs_scale=v_sc[a][:, cols],
+                        start=(a == 0),
+                        stop=(a == PASSES - 1),
+                    )
+                nc.scalar.activation(traits[t][:, cols], bank[:], ACT.Tanh)
 
-        def tanh_out(bank, t, s):
-            nc.scalar.activation(traits[t][:, s * BANK : (s + 1) * BANK], bank[:], ACT.Tanh)
+        first_product(0)
 
-        for s in range(SLICES):
-            bank = psum.tile([P, BANK], F32, name=f"bank{s}")
-            for a in range(PASSES):
-                first_pass(bank, 0, s, a)
-            tanh_out(bank, 0, s)
+        w_codes = [keep.tile([P, HALF_N], U32, name=f"w_codes{piece}", align_bytes=64) for piece in range(PIECES)]
+        w_sc = [keep.tile([P, HALF_N], U8, name=f"w_sc{piece}", align_bytes=64) for piece in range(PIECES)]
 
-        w_codes = [keep.tile([P, HALF_N], U32, name=f"w_codes{i}", align_bytes=64) for i in range(4)]
-        w_sc = [keep.tile([P, HALF_N], U8, name=f"w_sc{i}", align_bytes=64) for i in range(4)]
-
-        def round_weights(piece, copy):
-            grouped = ring.tile([P, HALF_N, PACK], BF16, name="w_grouped", align_bytes=64)
-            dst, src = interleave_views(grouped[:], w_raw[piece][:])
-            copy(dst, src)
-            return grouped
-
-        def quantize_weights(piece, grouped):
-            nc.vector.quantize_mx(
-                w_codes[piece][:].bitcast(FP8X4), w_sc[piece][:], grouped[:].rearrange("p c t -> p (c t)")
-            )
-
-        rest = PACK - 1
-        later = keep.tile([P, PASSES * rest * 3 * P], U8, name="later", tag="tab1", align_bytes=64)
-        split = PASSES * rest * 2 * P
-        later_codes = later[:, 0:split].rearrange("p (a t c) -> p a t c", a=PASSES, t=rest)
-        later_sc = later[:, split:].rearrange("p (a t c) -> p a t c", a=PASSES, t=rest)
-        nc.vector.tensor_copy(later_codes.bitcast(U16), w1_words_by_t[:, :, 1:PACK, :])
-        nc.vector.tensor_copy(later_sc, w1_sc_by_t[:, :, 1:PACK, :])
+        later_slots = PACK - 1
+        code_bytes = PASSES * later_slots * 2 * P
+        scale_bytes = PASSES * later_slots * P
+        later = keep.tile([P, code_bytes + scale_bytes], U8, name="later", tag="tab1", align_bytes=64)
+        later_codes = later[:, 0:code_bytes].rearrange("p (a t c) -> p a t c", a=PASSES, t=later_slots)
+        later_sc = later[:, code_bytes:].rearrange("p (a t c) -> p a t c", a=PASSES, t=later_slots)
+        nc.vector.tensor_copy(later_codes.bitcast(U16), w1_words_by_slot[:, :, 1:PACK, :])
+        nc.vector.tensor_copy(later_sc, w1_sc_by_slot[:, :, 1:PACK, :])
         for t in range(1, PACK):
             w1_codes[t] = later_codes[:, :, t - 1, :]
             w1_sc[t] = later_sc[:, :, t - 1, :]
-        w4_sc = zeroed_bytes("w4_sc", [P, N], tag="w1_sc_raw")
-        for quad in range(4):
-            nc.sync.dma_start(
-                w4_sc[32 * quad : 32 * quad + 4, :].bitcast(I32),
-                w4_scales[0, 4 * quad : 4 * quad + 4, :].bitcast(I32),
-            )
+
+        w4_sc = zeroed_scales("w4_sc", [P, N], "w1_sc_raw")
+        for quad in range(QUADS):
+            rows = w4_scales[0, SCALE_ROWS * quad : SCALE_ROWS * (quad + 1), :]
+            nc.sync.dma_start(w4_sc[scale_rows(quad), :].bitcast(I32), rows.bitcast(I32))
+
+        def round_side_by_side(name, by_slot):
+            grouped = ring.tile([P, by_slot.shape[2], PACK], BF16, name=name, align_bytes=64)
+            nc.scalar.copy(grouped[:], by_slot.rearrange("p t c -> p c t"))
+            return grouped[:].rearrange("p c t -> p (c t)")
 
         pairs = [keep.tile([P, PAIRS], F32, name=f"pairs{t}") for t in range(PACK)]
         site = [keep.tile([P, KEPT], F32, name=f"site{t}") for t in range(PACK)]
         for t in range(PACK):
-            nxt = t + 1
-            if nxt < PACK:
-                for s in range(SLICES):
-                    bank = psum.tile([P, BANK], F32, name=f"bank{s}")
-                    for a in range(PASSES):
-                        first_pass(bank, nxt, s, a)
-                    tanh_out(bank, nxt, s)
+            if t + 1 < PACK:
+                first_product(t + 1)
             left = ring.tile([P, PAIRS], F32, name="left")
             nc.vector.tensor_tensor(left[:], traits[t][:].indirect(pos1_t[:]), pair_gain[t][:], ALU.mult)
             nc.vector.tensor_tensor(site[t][:], traits[t][:].indirect(pos4_t[:]), site_gain[t][:], ALU.mult)
-            grouped = round_weights(t, nc.scalar.copy)
+            w_rounded = round_side_by_side("w_grouped", w_raw[t][:])
             nc.vector.tensor_tensor(pairs[t][:], traits[t][:].indirect(pos2_t[:]), left[:], ALU.mult)
-            quantize_weights(t, grouped)
+            nc.vector.quantize_mx(w_codes[t][:].bitcast(FP8X4), w_sc[t][:], w_rounded)
 
-        out_v = out.rearrange("(m p) j -> p m j", p=P)
-        chunks = KEPT // CHUNK
-        cstep = CHUNK // PER_COLUMN
+        out_tiles = out.rearrange("(m p) j -> p m j", p=P)
+        chunk_columns = CHUNK // PER_COLUMN
+        half_width = HALF_TILES * CHUNK
 
-        def kept(c):
-            planes = ring.tile([P, PACK, CHUNK], F32, name="kept_planes")
+        def kept_pairs(c):
+            a2 = ring.tile([P, PACK, CHUNK], F32, name="kept_planes")
             for t in range(PACK):
                 nc.vector.tensor_tensor(
-                    planes[:, t, :],
-                    pairs[t][:].indirect(pos3_t[:, c * cstep : (c + 1) * cstep]),
+                    a2[:, t, :],
+                    pairs[t][:].indirect(pos3_t[:, c * chunk_columns : (c + 1) * chunk_columns]),
                     site[t][:, c * CHUNK : (c + 1) * CHUNK],
                     ALU.subtract,
                 )
-            grouped = ring.tile([P, CHUNK, PACK], BF16, name="kept_grouped", align_bytes=64)
-            dst, src = interleave_views(grouped[:], planes[:])
-            if c < chunks - 1:
-                nc.scalar.copy(dst, src)
-            else:
-                nc.vector.tensor_copy(dst, src)
-            return grouped
+            return round_side_by_side("kept_grouped", a2[:])
 
-        def scores(c, grouped):
+        def scores(c, a2_rounded):
             codes = ring.tile([P, CHUNK], U32, name="kept_codes", align_bytes=64)
             scales = ring.tile([P, CHUNK], U8, name="kept_sc", align_bytes=64)
-            nc.vector.quantize_mx(codes[:].bitcast(FP8X4), scales[:], grouped[:].rearrange("p c t -> p (c t)"))
-            banks = []
-            for half in range(2):
-                trio = []
-                for which in range(3):
-                    bank = psum.tile([P, BANK], F32, name=f"bank{(6 * c + 3 * half + which) % 8}")
-                    for m in range(3):
-                        if which < 2:
-                            piece = 2 * half + which
-                            cols = slice(m * P, (m + 1) * P)
-                            lhs, lhs_sc = w_codes[piece][:, cols], w_sc[piece][:, cols]
-                        else:
-                            cols = slice(half * HALF_N + m * P, half * HALF_N + (m + 1) * P)
-                            lhs, lhs_sc = w4_codes[:, cols], w4_sc[:, cols]
-                        nc.tensor.matmul_mx(
-                            bank[:, m * CHUNK : (m + 1) * CHUNK],
-                            lhsT=lhs.bitcast(FP8X4),
-                            lhsT_scale=lhs_sc,
-                            rhs=codes[:].bitcast(FP8X4),
-                            rhs_scale=scales[:],
-                            start=True,
-                            stop=True,
-                        )
-                    trio.append(bank)
-                banks.append(trio)
-            return banks
+            nc.vector.quantize_mx(codes[:].bitcast(FP8X4), scales[:], a2_rounded)
+            y = {}
+            for place, (half, w) in enumerate(SCORE_ORDER):
+                bank = psum.tile([P, BANK], F32, name=f"bank{(len(SCORE_ORDER) * c + place) % BANKS}")
+                if w < 2:
+                    half_codes, half_sc = w_codes[2 * half + w][:], w_sc[2 * half + w][:]
+                else:
+                    half_cols = slice(half * HALF_N, (half + 1) * HALF_N)
+                    half_codes, half_sc = w4_codes[:, half_cols], w4_sc[:, half_cols]
+                for m in range(HALF_TILES):
+                    cols = slice(m * P, (m + 1) * P)
+                    nc.tensor.matmul_mx(
+                        bank[:, m * CHUNK : (m + 1) * CHUNK],
+                        lhsT=half_codes[:, cols].bitcast(FP8X4),
+                        lhsT_scale=half_sc[:, cols],
+                        rhs=codes[:].bitcast(FP8X4),
+                        rhs_scale=scales[:],
+                        start=True,
+                        stop=True,
+                    )
+                y[half, w] = bank[:, 0:half_width]
+            return y
 
-        def finish(c, banks):
-            width = 3 * CHUNK
+        def finish(c, y):
             larger = []
             for half in range(2):
-                y2 = ring.tile([P, width], F32, name="y2")
-                nc.scalar.copy(y2[:], banks[half][0][:, 0:width])
-                best = ring.tile([P, width], F32, name="best")
-                nc.vector.tensor_tensor(best[:], banks[half][1][:, 0:width], y2[:], ALU.max)
+                y2 = ring.tile([P, half_width], F32, name="y2")
+                nc.scalar.copy(y2[:], y[half, 0])
+                best = ring.tile([P, half_width], F32, name="best")
+                nc.vector.tensor_tensor(best[:], y[half, 1], y2[:], ALU.max)
                 larger.append(best)
             for half in range(2):
-                result = ring.tile([P, 3, CHUNK], F32, name="result", bufs=4)
-                nc.vector.tensor_tensor(
-                    result[:].rearrange("p m j -> p (m j)"), banks[half][2][:, 0:width], larger[half][:], ALU.add
-                )
-                nc.sync.dma_start(out_v[:, 3 * half : 3 * half + 3, c * CHUNK : (c + 1) * CHUNK], result[:])
+                result = ring.tile([P, HALF_TILES, CHUNK], F32, name="result", bufs=4)
+                nc.vector.tensor_tensor(result[:].rearrange("p m j -> p (m j)"), y[half, 2], larger[half][:], ALU.add)
+                tiles = slice(HALF_TILES * half, HALF_TILES * (half + 1))
+                nc.sync.dma_start(out_tiles[:, tiles, c * CHUNK : (c + 1) * CHUNK], result[:])
 
-        grouped = {0: kept(0)}
-        banks = {}
-        for c in range(chunks):
-            if c + 1 < chunks:
-                grouped[c + 1] = kept(c + 1)
+        rounded = {0: kept_pairs(0)}
+        products = {}
+        for c in range(CHUNKS):
+            if c + 1 < CHUNKS:
+                rounded[c + 1] = kept_pairs(c + 1)
             if c > 0:
-                finish(c - 1, banks[c - 1])
-            banks[c] = scores(c, grouped[c])
-        finish(chunks - 1, banks[chunks - 1])
+                finish(c - 1, products[c - 1])
+            products[c] = scores(c, rounded[c])
+        finish(CHUNKS - 1, products[CHUNKS - 1])

from contextlib import ExitStack

import concourse.mybir as mybir

K, T, S, PAIRS, KEPT, H, N = 1024, 4096, 2048, 1024, 512, 512, 768
FLOPS = 2 * K * H * S + 3 * 2 * H * N * KEPT

F32 = mybir.dt.float32
BF16 = mybir.dt.bfloat16
I32 = mybir.dt.int32
U32 = mybir.dt.uint32
U16 = mybir.dt.uint16
U8 = mybir.dt.uint8
FP8X4 = mybir.dt.float8_e4m3fn_x4
FP4X4 = mybir.dt.float4_e2m1fn_x4
ALU = mybir.AluOpType
ACT = mybir.ActivationFunctionType

P = 128
QUAD = 32
QUADS = P // QUAD
SCALE_ROWS = 4
PACK = 4
PASSES = K // (P * PACK)
BANK = 512
BANKS = 8
SLICES = S // BANK
PER_COLUMN = 16
HALF_N = N // 2
HALF_TILES = HALF_N // P
PIECES = 4
CHUNK = 128
CHUNKS = KEPT // CHUNK
SCORE_ORDER = [(half, w) for half in range(2) for w in range(2)] + [(half, 2) for half in range(2)]


def tile_list_tusk_pair_linking_kernel(
    tc, tab_words, tab_scales, offs, pos1, pos2, pos3, pos4, w1_words, w1_scales,
    gain, pgain, w2, w3, w4_words, w4_scales, out,
):
    nc = tc.nc
    with ExitStack() as ctx:
        lists = ctx.enter_context(tc.tile_pool(name="lists", bufs=1))
        keep = ctx.enter_context(tc.tile_pool(name="keep", bufs=1))
        ring = ctx.enter_context(tc.tile_pool(name="ring", bufs=2))
        psum = ctx.enter_context(tc.psum_pool(name="psum", bufs=1))

        def load_list(name, src):
            tile = lists.tile(list(src.shape), U16, name=name)
            nc.sync.dma_start(tile[:], src)
            return tile

        def zeroed_scales(name, shape, tag):
            tile = keep.tile(shape, U8, name=name, tag=tag, align_bytes=64)
            flat = tile[:] if len(shape) == 2 else tile[:].rearrange("p a c -> p (a c)")
            nc.vector.memset(flat.bitcast(I32), 0)
            return tile

        def scale_rows(quad):
            return slice(QUAD * quad, QUAD * quad + SCALE_ROWS)

        tab_sc = keep.tile([P, T], U8, name="tab_sc")
        nc.sync.dma_start(tab_sc[0:QUAD, :].bitcast(I32), tab_scales.rearrange("a q t -> (a q) t").bitcast(I32))
        nc.vector.memset(tab_sc[QUAD : 2 * QUAD, :].bitcast(I32), 0)
        nc.gpsimd.memset(tab_sc[2 * QUAD : P, :].bitcast(I32), 0)
        offs_t = load_list("offs_t", offs)

        gain_t = keep.tile([P, PACK], F32, name="gain_t")
        nc.sync.dma_start(gain_t[:], gain.rearrange("(p t) -> p t", t=PACK))
        pgain_t = keep.tile([P, PACK], F32, name="pgain_t")
        nc.sync.dma_start(pgain_t[:], pgain.rearrange("(p t) -> p t", t=PACK))
        both_gains = keep.tile([P, PACK], F32, name="both_gains")
        pair_gain = [keep.tile([P, PAIRS], F32, name=f"pair_gain{t}") for t in range(PACK)]
        site_gain = [keep.tile([P, KEPT], F32, name=f"site_gain{t}") for t in range(PACK)]
        for t in range(PACK):
            nc.scalar.activation(both_gains[:, t : t + 1], pgain_t[:, t : t + 1], ACT.Copy, scale=gain_t[:, t : t + 1])
        for t in range(PACK):
            nc.scalar.activation(
                pair_gain[t][:], both_gains[:, t : t + 1].to_broadcast([P, PAIRS]), ACT.Copy, scale=gain_t[:, t : t + 1]
            )
            nc.scalar.copy(site_gain[t][:], gain_t[:, t : t + 1].to_broadcast([P, KEPT]))

        w1_raw = keep.tile([P, PASSES, 2 * H], U8, name="w1_raw")
        tab = [keep.tile([P, T], I32, name=f"tab{a}", tag=f"tab{a}", align_bytes=64) for a in range(PASSES)]
        nc.sync.dma_start(tab[0][:], tab_words[0].rearrange("p t i -> p (t i)").bitcast(I32))
        nc.sync.dma_start(w1_raw[:].bitcast(I32), w1_words.rearrange("a p c -> p a c").bitcast(I32))
        w1_sc_raw = zeroed_scales("w1_sc_raw", [P, PASSES, H], "w1_sc_raw")
        for quad in range(QUADS):
            rows = w1_scales[:, SCALE_ROWS * quad : SCALE_ROWS * (quad + 1), :]
            nc.sync.dma_start(
                w1_sc_raw[scale_rows(quad), :, :].bitcast(I32), rows.rearrange("a i c -> i a c").bitcast(I32)
            )
        nc.sync.dma_start(tab[1][:], tab_words[1].rearrange("p t i -> p (t i)").bitcast(I32))
        v_sc = [zeroed_scales(f"v_sc{a}", [P, S], f"v_sc{a}") for a in range(PASSES)]

        picked_sc = keep.tile([P, S], U8, name="picked_sc")
        nc.vector.tensor_copy(picked_sc[:], tab_sc[:].indirect(offs_t[:]))
        for a in range(PASSES):
            for quad in range(QUADS):
                row = SCALE_ROWS * (QUADS * a + quad)
                nc.sync.dma_start(
                    v_sc[a][scale_rows(quad), :].bitcast(I32), picked_sc[row : row + SCALE_ROWS, :].bitcast(I32)
                )

        w1_words_by_slot = w1_raw[:].bitcast(U16).rearrange("p a (q t) -> p a t q", t=PACK)
        w1_sc_by_slot = w1_sc_raw[:].rearrange("p a (q t) -> p a t q", t=PACK)
        first_codes = keep.tile([P, PASSES, 1, 2 * P], U8, name="first_codes", align_bytes=64)
        nc.vector.tensor_copy(first_codes[:].bitcast(U16), w1_words_by_slot[:, :, 0:1, :])
        first_sc = keep.tile([P, PASSES, 1, P], U8, name="first_sc", align_bytes=64)
        nc.vector.tensor_copy(first_sc[:], w1_sc_by_slot[:, :, 0:1, :])
        w1_codes = {0: first_codes[:, :, 0, :]}
        w1_sc = {0: first_sc[:, :, 0, :]}

        v0 = keep.tile([P, S], U32, name="v0", align_bytes=64)
        nc.vector.tensor_copy(v0[:], tab[0][:].bitcast(U32).indirect(offs_t[:]))
        slice_columns = BANK // PER_COLUMN
        v1 = [keep.tile([P, BANK], U32, name=f"v1_{s}", align_bytes=64) for s in range(SLICES)]
        for s in range(SLICES):
            slice_offs = offs_t[:, s * slice_columns : (s + 1) * slice_columns]
            nc.vector.tensor_copy(v1[s][:], tab[1][:].bitcast(U32).indirect(slice_offs))

        pos1_t = load_list("pos1_t", pos1)
        pos4_t = load_list("pos4_t", pos4)
        pos2_t = load_list("pos2_t", pos2)
        pos3_t = load_list("pos3_t", pos3)
        w4_codes = keep.tile([P, N], I32, name="w4_codes", align_bytes=64)
        nc.sync.dma_start(w4_codes[:], w4_words[0].rearrange("p c i -> p (c i)").bitcast(I32))
        w_raw = []
        for piece in range(PIECES):
            half, w = divmod(piece, 2)
            src = (w2, w3)[w][:, half * HALF_N : (half + 1) * HALF_N]
            raw = keep.tile([P, PACK, HALF_N], F32, name=f"w_raw{piece}")
            nc.sync.dma_start(raw[:], src.rearrange("(p t) n -> p t n", t=PACK))
            w_raw.append(raw)

        traits = [keep.tile([P, S], F32, name=f"traits{t}") for t in range(PACK)]

        def first_product(t):
            for s in range(SLICES):
                cols = slice(s * BANK, (s + 1) * BANK)
                bank = psum.tile([P, BANK], F32, name=f"bank{s}")
                for a, words in enumerate((v0[:, cols], v1[s][:])):
                    nc.tensor.matmul_mx(
                        bank[:],
                        lhsT=w1_codes[t][:, a, :].bitcast(FP4X4),
                        lhsT_scale=w1_sc[t][:, a, :],
                        rhs=words.bitcast(FP8X4),
                        rhs_scale=v_sc[a][:, cols],
                        start=(a == 0),
                        stop=(a == PASSES - 1),
                    )
                nc.scalar.activation(traits[t][:, cols], bank[:], ACT.Tanh)

        first_product(0)

        w_codes = [keep.tile([P, HALF_N], U32, name=f"w_codes{piece}", align_bytes=64) for piece in range(PIECES)]
        w_sc = [keep.tile([P, HALF_N], U8, name=f"w_sc{piece}", align_bytes=64) for piece in range(PIECES)]

        later_slots = PACK - 1
        code_bytes = PASSES * later_slots * 2 * P
        scale_bytes = PASSES * later_slots * P
        later = keep.tile([P, code_bytes + scale_bytes], U8, name="later", tag="tab1", align_bytes=64)
        later_codes = later[:, 0:code_bytes].rearrange("p (a t c) -> p a t c", a=PASSES, t=later_slots)
        later_sc = later[:, code_bytes:].rearrange("p (a t c) -> p a t c", a=PASSES, t=later_slots)
        nc.vector.tensor_copy(later_codes.bitcast(U16), w1_words_by_slot[:, :, 1:PACK, :])
        nc.vector.tensor_copy(later_sc, w1_sc_by_slot[:, :, 1:PACK, :])
        for t in range(1, PACK):
            w1_codes[t] = later_codes[:, :, t - 1, :]
            w1_sc[t] = later_sc[:, :, t - 1, :]

        w4_sc = zeroed_scales("w4_sc", [P, N], "w1_sc_raw")
        for quad in range(QUADS):
            rows = w4_scales[0, SCALE_ROWS * quad : SCALE_ROWS * (quad + 1), :]
            nc.sync.dma_start(w4_sc[scale_rows(quad), :].bitcast(I32), rows.bitcast(I32))

        def round_side_by_side(name, by_slot):
            grouped = ring.tile([P, by_slot.shape[2], PACK], BF16, name=name, align_bytes=64)
            nc.scalar.copy(grouped[:], by_slot.rearrange("p t c -> p c t"))
            return grouped[:].rearrange("p c t -> p (c t)")

        pairs = [keep.tile([P, PAIRS], F32, name=f"pairs{t}") for t in range(PACK)]
        site = [keep.tile([P, KEPT], F32, name=f"site{t}") for t in range(PACK)]
        for t in range(PACK):
            if t + 1 < PACK:
                first_product(t + 1)
            left = ring.tile([P, PAIRS], F32, name="left")
            nc.vector.tensor_tensor(left[:], traits[t][:].indirect(pos1_t[:]), pair_gain[t][:], ALU.mult)
            nc.vector.tensor_tensor(site[t][:], traits[t][:].indirect(pos4_t[:]), site_gain[t][:], ALU.mult)
            w_rounded = round_side_by_side("w_grouped", w_raw[t][:])
            nc.vector.tensor_tensor(pairs[t][:], traits[t][:].indirect(pos2_t[:]), left[:], ALU.mult)
            nc.vector.quantize_mx(w_codes[t][:].bitcast(FP8X4), w_sc[t][:], w_rounded)

        out_tiles = out.rearrange("(m p) j -> p m j", p=P)
        chunk_columns = CHUNK // PER_COLUMN
        half_width = HALF_TILES * CHUNK

        def kept_pairs(c):
            a2 = ring.tile([P, PACK, CHUNK], F32, name="kept_planes")
            for t in range(PACK):
                nc.vector.tensor_tensor(
                    a2[:, t, :],
                    pairs[t][:].indirect(pos3_t[:, c * chunk_columns : (c + 1) * chunk_columns]),
                    site[t][:, c * CHUNK : (c + 1) * CHUNK],
                    ALU.subtract,
                )
            return round_side_by_side("kept_grouped", a2[:])

        def scores(c, a2_rounded):
            codes = ring.tile([P, CHUNK], U32, name="kept_codes", align_bytes=64)
            scales = ring.tile([P, CHUNK], U8, name="kept_sc", align_bytes=64)
            nc.vector.quantize_mx(codes[:].bitcast(FP8X4), scales[:], a2_rounded)
            y = {}
            for place, (half, w) in enumerate(SCORE_ORDER):
                bank = psum.tile([P, BANK], F32, name=f"bank{(len(SCORE_ORDER) * c + place) % BANKS}")
                if w < 2:
                    half_codes, half_sc = w_codes[2 * half + w][:], w_sc[2 * half + w][:]
                else:
                    half_cols = slice(half * HALF_N, (half + 1) * HALF_N)
                    half_codes, half_sc = w4_codes[:, half_cols], w4_sc[:, half_cols]
                for m in range(HALF_TILES):
                    cols = slice(m * P, (m + 1) * P)
                    nc.tensor.matmul_mx(
                        bank[:, m * CHUNK : (m + 1) * CHUNK],
                        lhsT=half_codes[:, cols].bitcast(FP8X4),
                        lhsT_scale=half_sc[:, cols],
                        rhs=codes[:].bitcast(FP8X4),
                        rhs_scale=scales[:],
                        start=True,
                        stop=True,
                    )
                y[half, w] = bank[:, 0:half_width]
            return y

        def finish(c, y):
            larger = []
            for half in range(2):
                y2 = ring.tile([P, half_width], F32, name="y2")
                nc.scalar.copy(y2[:], y[half, 0])
                best = ring.tile([P, half_width], F32, name="best")
                nc.vector.tensor_tensor(best[:], y[half, 1], y2[:], ALU.max)
                larger.append(best)
            for half in range(2):
                result = ring.tile([P, HALF_TILES, CHUNK], F32, name="result", bufs=4)
                nc.vector.tensor_tensor(result[:].rearrange("p m j -> p (m j)"), y[half, 2], larger[half][:], ALU.add)
                tiles = slice(HALF_TILES * half, HALF_TILES * (half + 1))
                nc.sync.dma_start(out_tiles[:, tiles, c * CHUNK : (c + 1) * CHUNK], result[:])

        rounded = {0: kept_pairs(0)}
        products = {}
        for c in range(CHUNKS):
            if c + 1 < CHUNKS:
                rounded[c + 1] = kept_pairs(c + 1)
            if c > 0:
                finish(c - 1, products[c - 1])
            products[c] = scores(c, rounded[c])
        finish(CHUNKS - 1, products[CHUNKS - 1])
